import numpy as np
import ml_dtypes


def mxq(x, axis, fmt="e4m3"):
    dtype, down = {"e4m3": (ml_dtypes.float8_e4m3fn, 7), "e5m2": (ml_dtypes.float8_e5m2, 14)}[fmt]
    v = np.moveaxis(np.asarray(x, np.float32).astype(ml_dtypes.bfloat16).astype(np.float64), axis, -1)
    blocks = v.reshape(v.shape[:-1] + (-1, 32))
    amax = np.abs(blocks).max(-1, keepdims=True)
    byte = np.maximum(np.where(amax > 0, np.frexp(amax)[1] - 1 + 127, 0) - down, 1)
    scale = np.exp2(byte - 127.0)
    codes = (blocks / scale).astype(np.float32).astype(dtype).astype(np.float64)
    return np.moveaxis((codes * scale).reshape(v.shape), -1, axis)


WIDE = False


def mx_kscale(k):
    if not WIDE:
        return np.ones(k)
    levels = np.array([10, -10, 5, -5, 0])
    if k % 512:
        return np.exp2(np.random.permutation(np.resize(levels, k // 32))).repeat(32)
    a = np.empty((k // 512, 16))
    for p in range(k // 512):
        a[p, :8] = np.random.permutation(np.resize(levels, 8))
        for g in range(8):
            far = levels[np.abs(levels - a[p, g]) >= 10]
            a[p, g + 8] = far[np.random.randint(len(far))]
    return np.exp2(a.ravel()).repeat(32)


def f64(x):
    return np.asarray(x).astype(np.float64)


def striped(idx):
    return np.tile(idx.reshape(-1, 16).T, (8, 1)).astype(np.uint16)


def unstriped(offs):
    return offs[:16].T.reshape(-1).astype(np.int64)


def pack_weight(w):
    k, n = w.shape
    w = f64(np.asarray(w, np.float32).astype(ml_dtypes.bfloat16)).reshape(k // 32, 32, n)
    amax = np.abs(w).max(1)
    byte = np.clip(np.where(amax > 0, np.frexp(amax)[1] - 1 + 127 - 7, 1), 1, 254)
    scaled = (w * np.exp2(127.0 - byte)[:, None, :]).reshape(k, n).astype(np.float32)
    words = np.ascontiguousarray(scaled.reshape(k // 512, 128, 4, n).transpose(0, 1, 3, 2)).astype(ml_dtypes.float8_e4m3fn).view(np.uint8)
    return words, np.ascontiguousarray(byte.astype(np.uint8).reshape(k // 512, 16, n))


def unpack_weight(words, scales):
    g, p, n, _ = words.shape
    vals = np.ascontiguousarray(words).view(ml_dtypes.float8_e4m3fn).astype(np.float64) * np.repeat(np.exp2(scales.astype(np.float64) - 127.0), 8, axis=1)[..., None]
    return vals.transpose(0, 1, 3, 2).reshape(g * 512, n)


K, T, S, N = 512, 2048, 1024, 256


def setup_inputs():
    n = np.random.standard_normal
    s = mx_kscale(K)[:, None]
    packed = pack_weight(n((K, T)) * s)
    return {
        "x_words": packed[0],
        "x_scales": packed[1],
        "w": (n((K, N)) / np.sqrt(K) / s).astype(np.float32),
        "gate": np.tile(np.random.uniform(0.2, 1.0, S), (N, 1)).astype(np.float32),
        "offs": striped(np.random.permutation(T)[:S]),
    }


def reference(x_words, x_scales, w, gate, offs):
    idx = unstriped(offs)
    xq = unpack_weight(x_words, x_scales)[:, idx]
    y = mxq(f64(w), 0, "e4m3").T @ xq
    out = np.zeros((N, T))
    out[:, idx] = f64(gate) * y
    return out

@@ -1,0 +1,112 @@
+from contextlib import ExitStack
+
+import concourse.mybir as mybir
+
+K, T, S, N = 512, 2048, 1024, 256
+FLOPS = 2 * K * S * N
+
+F32 = mybir.dt.float32
+BF16 = mybir.dt.bfloat16
+I32 = mybir.dt.int32
+U32 = mybir.dt.uint32
+U16 = mybir.dt.uint16
+U8 = mybir.dt.uint8
+FP8X4 = mybir.dt.float8_e4m3fn_x4
+MULT = mybir.AluOpType.mult
+
+P = 128
+PACK = 4
+HALF = S // 2
+PER_COL = 16
+
+
+def tile_picked_depth_lin_none_sub_p_kernel(tc, x_words, x_scales, w, gate, offs, out):
+    nc = tc.nc
+    with ExitStack() as ctx:
+        keep = ctx.enter_context(tc.tile_pool(name="keep", bufs=1))
+        psum = ctx.enter_context(tc.psum_pool(name="psum", bufs=1))
+
+        offsets = keep.tile([P, S // PER_COL], U16, name="offsets")
+        nc.sync.dma_start(offsets[:], offs)
+
+        scale_table = keep.tile([P, T], U8, name="scale_table", align_bytes=64)
+        nc.vector.memset(scale_table[:].bitcast(I32), 0)
+        for q in range(4):
+            nc.scalar.dma_start(
+                scale_table[32 * q : 32 * q + 4, :].bitcast(I32),
+                x_scales[0, 4 * q : 4 * q + 4, :].bitcast(I32),
+            )
+
+        word_table = keep.tile([P, T], I32, name="word_table", align_bytes=64)
+        nc.sync.dma_start(word_table[:], x_words[0].rearrange("p c r -> p (c r)").bitcast(I32))
+
+        w_raw = keep.tile([P, PACK, N], F32, name="w_raw", align_bytes=64)
+        nc.sync.dma_start(w_raw[:], w.rearrange("(p j) n -> p j n", j=PACK))
+
+        gates = keep.tile([P, S], F32, name="gates", align_bytes=64)
+        nc.sync.dma_start(gates[:], gate[0:P, :])
+
+        windows = [keep.tile([P, T], F32, name="window%d" % b, align_bytes=64) for b in range(2)]
+        for b in range(2):
+            nc.vector.memset(windows[b][:], 0.0)
+
+        picked_scales = keep.tile([P, S], U8, name="picked_scales", align_bytes=64)
+        nc.vector.tensor_copy(picked_scales[:], scale_table[:].indirect(offsets[:]))
+
+        picked_words = [keep.tile([P, HALF], U32, name="picked_words%d" % h, align_bytes=64) for h in range(2)]
+
+        def entries(lo, hi):
+            return offsets[:, lo // PER_COL : hi // PER_COL]
+
+        def gather_words(h):
+            nc.vector.tensor_copy(
+                picked_words[h][:], word_table[:].bitcast(U32).indirect(entries(h * HALF, (h + 1) * HALF))
+            )
+
+        w_grouped = [keep.tile([P, P, PACK], BF16, name="w_grouped%d" % b, align_bytes=64) for b in range(2)]
+        w_codes = [keep.tile([P, P], U32, name="w_codes%d" % b, align_bytes=64) for b in range(2)]
+        w_scales = [keep.tile([P, P], U8, name="w_scales%d" % b, align_bytes=64) for b in range(2)]
+
+        def cast_w(b):
+            nc.scalar.copy(w_grouped[b][:], w_raw[:, :, b * P : (b + 1) * P].rearrange("p j n -> p n j"))
+
+        def quantize_w(b):
+            nc.vector.quantize_mx(
+                out=w_codes[b][:].bitcast(FP8X4),
+                scales=w_scales[b][:],
+                in_=w_grouped[b][:].rearrange("p n j -> p (n j)"),
+            )
+
+        y0 = [keep.tile([P, HALF], F32, name="y0_%d" % h, align_bytes=64) for h in range(2)]
+        y1 = keep.tile([P, S], F32, name="y1", align_bytes=64)
+
+        def product(b, h):
+            acc = psum.tile([P, HALF], F32, name="acc%d%d" % (b, h))
+            nc.tensor.matmul_mx(
+                out=acc[:],
+                lhsT=w_codes[b][:].bitcast(FP8X4),
+                lhsT_scale=w_scales[b][:],
+                rhs=picked_words[h][:].bitcast(FP8X4),
+                rhs_scale=picked_scales[:, h * HALF : (h + 1) * HALF],
+                start=True,
+                stop=True,
+            )
+            dst = y0[h][:] if b == 0 else y1[:, h * HALF : (h + 1) * HALF]
+            nc.scalar.copy(dst, acc[:])
+
+        cast_w(0)
+        cast_w(1)
+        gather_words(0)
+        quantize_w(0)
+        product(0, 0)
+        gather_words(1)
+        quantize_w(1)
+        product(1, 0)
+        product(1, 1)
+        product(0, 1)
+
+        nc.vector.tensor_tensor(windows[0][:].indirect(entries(0, HALF)), y0[0][:], gates[:, 0:HALF], MULT)
+        nc.vector.tensor_tensor(windows[1][:].indirect(offsets[:]), y1[:], gates[:], MULT)
+        nc.sync.dma_start(out[P : 2 * P, :], windows[1][:])
+        nc.vector.tensor_tensor(windows[0][:].indirect(entries(HALF, S)), y0[1][:], gates[:, HALF:S], MULT)
+        nc.sync.dma_start(out[0:P, :], windows[0][:])

@@ -16,8 +16,9 @@ MULT = mybir.AluOpType.mult
 
 P = 128
 PACK = 4
-HALF = S // 2
 PER_COL = 16
+BANK = 512
+FIRST = 256
 
 
 def tile_picked_depth_lin_none_sub_p_kernel(tc, x_words, x_scales, w, gate, offs, out):
@@ -32,19 +33,19 @@ def tile_picked_depth_lin_none_sub_p_kernel(tc, x_words, x_scales, w, gate, offs
         scale_table = keep.tile([P, T], U8, name="scale_table", align_bytes=64)
         nc.vector.memset(scale_table[:].bitcast(I32), 0)
         for q in range(4):
-            nc.scalar.dma_start(
+            nc.sync.dma_start(
                 scale_table[32 * q : 32 * q + 4, :].bitcast(I32),
                 x_scales[0, 4 * q : 4 * q + 4, :].bitcast(I32),
             )
 
-        word_table = keep.tile([P, T], I32, name="word_table", align_bytes=64)
-        nc.sync.dma_start(word_table[:], x_words[0].rearrange("p c r -> p (c r)").bitcast(I32))
-
         w_raw = keep.tile([P, PACK, N], F32, name="w_raw", align_bytes=64)
-        nc.sync.dma_start(w_raw[:], w.rearrange("(p j) n -> p j n", j=PACK))
+        nc.scalar.dma_start(w_raw[:], w.rearrange("(p j) n -> p j n", j=PACK))
+
+        word_table = keep.tile([P, T], I32, name="word_table", align_bytes=64)
+        nc.scalar.dma_start(word_table[:], x_words[0].rearrange("p c r -> p (c r)").bitcast(I32))
 
         gates = keep.tile([P, S], F32, name="gates", align_bytes=64)
-        nc.sync.dma_start(gates[:], gate[0:P, :])
+        nc.scalar.dma_start(gates[:], gate[0:P, :])
 
         windows = [keep.tile([P, T], F32, name="window%d" % b, align_bytes=64) for b in range(2)]
         for b in range(2):
@@ -53,60 +54,43 @@ def tile_picked_depth_lin_none_sub_p_kernel(tc, x_words, x_scales, w, gate, offs
         picked_scales = keep.tile([P, S], U8, name="picked_scales", align_bytes=64)
         nc.vector.tensor_copy(picked_scales[:], scale_table[:].indirect(offsets[:]))
 
-        picked_words = [keep.tile([P, HALF], U32, name="picked_words%d" % h, align_bytes=64) for h in range(2)]
+        w_grouped = keep.tile([P, N, PACK], BF16, name="w_grouped", tag="staging", align_bytes=64)
+        w_codes = keep.tile([P, N], U32, name="w_codes", align_bytes=64)
+        w_scales = keep.tile([P, N], U8, name="w_scales", align_bytes=64)
+        nc.scalar.copy(w_grouped[:], w_raw[:].rearrange("p j n -> p n j"))
+        nc.vector.quantize_mx(
+            out=w_codes[:].bitcast(FP8X4),
+            scales=w_scales[:],
+            in_=w_grouped[:].rearrange("p n j -> p (n j)"),
+        )
+
+        pieces = [(0, FIRST), (FIRST, S)]
 
         def entries(lo, hi):
             return offsets[:, lo // PER_COL : hi // PER_COL]
 
-        def gather_words(h):
-            nc.vector.tensor_copy(
-                picked_words[h][:], word_table[:].bitcast(U32).indirect(entries(h * HALF, (h + 1) * HALF))
-            )
+        picked_words = keep.tile([P, S], U32, name="picked_words", tag="staging", align_bytes=64)
+        y = {}
+        for h, (lo, hi) in enumerate(pieces):
+            nc.vector.tensor_copy(picked_words[:, lo:hi], word_table[:].bitcast(U32).indirect(entries(lo, hi)))
+            for b in range(2):
+                y[h, b] = keep.tile([P, hi - lo], F32, name="y%d%d" % (h, b), align_bytes=64)
+                for c0 in range(0, hi - lo, BANK):
+                    c1 = min(c0 + BANK, hi - lo)
+                    acc = psum.tile([P, c1 - c0], F32, name="acc%d%d%d" % (h, b, c0))
+                    nc.tensor.matmul_mx(
+                        out=acc[:],
+                        lhsT=w_codes[:, b * P : (b + 1) * P].bitcast(FP8X4),
+                        lhsT_scale=w_scales[:, b * P : (b + 1) * P],
+                        rhs=picked_words[:, lo + c0 : lo + c1].bitcast(FP8X4),
+                        rhs_scale=picked_scales[:, lo + c0 : lo + c1],
+                        start=True,
+                        stop=True,
+                    )
+                    nc.scalar.copy(y[h, b][:, c0:c1], acc[:])
 
-        w_grouped = [keep.tile([P, P, PACK], BF16, name="w_grouped%d" % b, align_bytes=64) for b in range(2)]
-        w_codes = [keep.tile([P, P], U32, name="w_codes%d" % b, align_bytes=64) for b in range(2)]
-        w_scales = [keep.tile([P, P], U8, name="w_scales%d" % b, align_bytes=64) for b in range(2)]
-
-        def cast_w(b):
-            nc.scalar.copy(w_grouped[b][:], w_raw[:, :, b * P : (b + 1) * P].rearrange("p j n -> p n j"))
-
-        def quantize_w(b):
-            nc.vector.quantize_mx(
-                out=w_codes[b][:].bitcast(FP8X4),
-                scales=w_scales[b][:],
-                in_=w_grouped[b][:].rearrange("p n j -> p (n j)"),
-            )
-
-        y0 = [keep.tile([P, HALF], F32, name="y0_%d" % h, align_bytes=64) for h in range(2)]
-        y1 = keep.tile([P, S], F32, name="y1", align_bytes=64)
-
-        def product(b, h):
-            acc = psum.tile([P, HALF], F32, name="acc%d%d" % (b, h))
-            nc.tensor.matmul_mx(
-                out=acc[:],
-                lhsT=w_codes[b][:].bitcast(FP8X4),
-                lhsT_scale=w_scales[b][:],
-                rhs=picked_words[h][:].bitcast(FP8X4),
-                rhs_scale=picked_scales[:, h * HALF : (h + 1) * HALF],
-                start=True,
-                stop=True,
-            )
-            dst = y0[h][:] if b == 0 else y1[:, h * HALF : (h + 1) * HALF]
-            nc.scalar.copy(dst, acc[:])
-
-        cast_w(0)
-        cast_w(1)
-        gather_words(0)
-        quantize_w(0)
-        product(0, 0)
-        gather_words(1)
-        quantize_w(1)
-        product(1, 0)
-        product(1, 1)
-        product(0, 1)
-
-        nc.vector.tensor_tensor(windows[0][:].indirect(entries(0, HALF)), y0[0][:], gates[:, 0:HALF], MULT)
-        nc.vector.tensor_tensor(windows[1][:].indirect(offsets[:]), y1[:], gates[:], MULT)
-        nc.sync.dma_start(out[P : 2 * P, :], windows[1][:])
-        nc.vector.tensor_tensor(windows[0][:].indirect(entries(HALF, S)), y0[1][:], gates[:, HALF:S], MULT)
-        nc.sync.dma_start(out[0:P, :], windows[0][:])
+        for h, (lo, hi) in enumerate(pieces):
+            for b in range(2):
+                nc.vector.tensor_tensor(windows[b][:].indirect(entries(lo, hi)), y[h, b][:], gates[:, lo:hi], MULT)
+                if h == len(pieces) - 1:
+                    nc.sync.dma_start(out[b * P : (b + 1) * P, :], windows[b][:])

@@ -30,6 +30,9 @@ def tile_picked_depth_lin_none_sub_p_kernel(tc, x_words, x_scales, w, gate, offs
         offsets = keep.tile([P, S // PER_COL], U16, name="offsets")
         nc.sync.dma_start(offsets[:], offs)
 
+        w_raw = keep.tile([P, PACK, N], F32, name="w_raw", align_bytes=64)
+        nc.sync.dma_start(w_raw[:], w.rearrange("(p j) n -> p j n", j=PACK))
+
         scale_table = keep.tile([P, T], U8, name="scale_table", align_bytes=64)
         nc.vector.memset(scale_table[:].bitcast(I32), 0)
         for q in range(4):
@@ -38,14 +41,11 @@ def tile_picked_depth_lin_none_sub_p_kernel(tc, x_words, x_scales, w, gate, offs
                 x_scales[0, 4 * q : 4 * q + 4, :].bitcast(I32),
             )
 
-        w_raw = keep.tile([P, PACK, N], F32, name="w_raw", align_bytes=64)
-        nc.scalar.dma_start(w_raw[:], w.rearrange("(p j) n -> p j n", j=PACK))
-
         word_table = keep.tile([P, T], I32, name="word_table", align_bytes=64)
-        nc.scalar.dma_start(word_table[:], x_words[0].rearrange("p c r -> p (c r)").bitcast(I32))
+        nc.sync.dma_start(word_table[:], x_words[0].rearrange("p c r -> p (c r)").bitcast(I32))
 
         gates = keep.tile([P, S], F32, name="gates", align_bytes=64)
-        nc.scalar.dma_start(gates[:], gate[0:P, :])
+        nc.sync.dma_start(gates[:], gate[0:P, :])
 
         windows = [keep.tile([P, T], F32, name="window%d" % b, align_bytes=64) for b in range(2)]
         for b in range(2):

@@ -30,8 +30,9 @@ def tile_picked_depth_lin_none_sub_p_kernel(tc, x_words, x_scales, w, gate, offs
         offsets = keep.tile([P, S // PER_COL], U16, name="offsets")
         nc.sync.dma_start(offsets[:], offs)
 
-        w_raw = keep.tile([P, PACK, N], F32, name="w_raw", align_bytes=64)
-        nc.sync.dma_start(w_raw[:], w.rearrange("(p j) n -> p j n", j=PACK))
+        w_rows = w.rearrange("(p j) n -> p j n", j=PACK)
+        w_raw = [keep.tile([P, PACK, P], F32, name="w_raw%d" % b, align_bytes=64) for b in range(2)]
+        nc.sync.dma_start(w_raw[0][:], w_rows[:, :, 0:P])
 
         scale_table = keep.tile([P, T], U8, name="scale_table", align_bytes=64)
         nc.vector.memset(scale_table[:].bitcast(I32), 0)
@@ -44,6 +45,8 @@ def tile_picked_depth_lin_none_sub_p_kernel(tc, x_words, x_scales, w, gate, offs
         word_table = keep.tile([P, T], I32, name="word_table", align_bytes=64)
         nc.sync.dma_start(word_table[:], x_words[0].rearrange("p c r -> p (c r)").bitcast(I32))
 
+        nc.sync.dma_start(w_raw[1][:], w_rows[:, :, P : 2 * P])
+
         gates = keep.tile([P, S], F32, name="gates", align_bytes=64)
         nc.sync.dma_start(gates[:], gate[0:P, :])
 
@@ -54,34 +57,42 @@ def tile_picked_depth_lin_none_sub_p_kernel(tc, x_words, x_scales, w, gate, offs
         picked_scales = keep.tile([P, S], U8, name="picked_scales", align_bytes=64)
         nc.vector.tensor_copy(picked_scales[:], scale_table[:].indirect(offsets[:]))
 
-        w_grouped = keep.tile([P, N, PACK], BF16, name="w_grouped", tag="staging", align_bytes=64)
-        w_codes = keep.tile([P, N], U32, name="w_codes", align_bytes=64)
-        w_scales = keep.tile([P, N], U8, name="w_scales", align_bytes=64)
-        nc.scalar.copy(w_grouped[:], w_raw[:].rearrange("p j n -> p n j"))
-        nc.vector.quantize_mx(
-            out=w_codes[:].bitcast(FP8X4),
-            scales=w_scales[:],
-            in_=w_grouped[:].rearrange("p n j -> p (n j)"),
-        )
+        w_grouped = [keep.tile([P, P, PACK], BF16, name="w_grouped%d" % b, align_bytes=64) for b in range(2)]
+        w_codes = [keep.tile([P, P], U32, name="w_codes%d" % b, align_bytes=64) for b in range(2)]
+        w_scales = [keep.tile([P, P], U8, name="w_scales%d" % b, align_bytes=64) for b in range(2)]
+        for b in range(2):
+            nc.scalar.copy(w_grouped[b][:], w_raw[b][:].rearrange("p j n -> p n j"))
+
+        def quantize_w(b):
+            nc.vector.quantize_mx(
+                out=w_codes[b][:].bitcast(FP8X4),
+                scales=w_scales[b][:],
+                in_=w_grouped[b][:].rearrange("p n j -> p (n j)"),
+            )
 
         pieces = [(0, FIRST), (FIRST, S)]
 
         def entries(lo, hi):
             return offsets[:, lo // PER_COL : hi // PER_COL]
 
-        picked_words = keep.tile([P, S], U32, name="picked_words", tag="staging", align_bytes=64)
+        picked_words = keep.tile([P, S], U32, name="picked_words", align_bytes=64)
+        quantize_w(0)
+        for lo, hi in pieces:
+            nc.vector.tensor_copy(picked_words[:, lo:hi], word_table[:].bitcast(U32).indirect(entries(lo, hi)))
+        quantize_w(1)
+
+        bank_of = {(0, 0, 0): 0, (0, 1, 0): 1, (1, 0, 0): 1, (1, 0, BANK): 2, (1, 1, 0): 1, (1, 1, BANK): 2}
         y = {}
         for h, (lo, hi) in enumerate(pieces):
-            nc.vector.tensor_copy(picked_words[:, lo:hi], word_table[:].bitcast(U32).indirect(entries(lo, hi)))
             for b in range(2):
                 y[h, b] = keep.tile([P, hi - lo], F32, name="y%d%d" % (h, b), align_bytes=64)
                 for c0 in range(0, hi - lo, BANK):
                     c1 = min(c0 + BANK, hi - lo)
-                    acc = psum.tile([P, c1 - c0], F32, name="acc%d%d%d" % (h, b, c0))
+                    acc = psum.tile([P, c1 - c0], F32, name="acc%d%d%d" % (h, b, c0), tag="bank%d" % bank_of[h, b, c0])
                     nc.tensor.matmul_mx(
                         out=acc[:],
-                        lhsT=w_codes[:, b * P : (b + 1) * P].bitcast(FP8X4),
-                        lhsT_scale=w_scales[:, b * P : (b + 1) * P],
+                        lhsT=w_codes[b][:].bitcast(FP8X4),
+                        lhsT_scale=w_scales[b][:],
                         rhs=picked_words[:, lo + c0 : lo + c1].bitcast(FP8X4),
                         rhs_scale=picked_scales[:, lo + c0 : lo + c1],
                         start=True,

@@ -34,7 +34,7 @@ def tile_picked_depth_lin_none_sub_p_kernel(tc, x_words, x_scales, w, gate, offs
         w_raw = [keep.tile([P, PACK, P], F32, name="w_raw%d" % b, align_bytes=64) for b in range(2)]
         nc.sync.dma_start(w_raw[0][:], w_rows[:, :, 0:P])
 
-        scale_table = keep.tile([P, T], U8, name="scale_table", align_bytes=64)
+        scale_table = keep.tile([P, T], U8, name="scale_table", tag="reused", align_bytes=64)
         nc.vector.memset(scale_table[:].bitcast(I32), 0)
         for q in range(4):
             nc.sync.dma_start(
@@ -51,14 +51,16 @@ def tile_picked_depth_lin_none_sub_p_kernel(tc, x_words, x_scales, w, gate, offs
         nc.sync.dma_start(gates[:], gate[0:P, :])
 
         windows = [keep.tile([P, T], F32, name="window%d" % b, align_bytes=64) for b in range(2)]
-        for b in range(2):
-            nc.vector.memset(windows[b][:], 0.0)
+        zero = keep.tile([P, 1], F32, name="zero")
+        nc.vector.memset(zero[:], 0.0)
+        nc.vector.memset(windows[0][:], 0.0)
+        nc.scalar.copy(windows[1][:], zero[:].to_broadcast([P, T]))
 
         picked_scales = keep.tile([P, S], U8, name="picked_scales", align_bytes=64)
         nc.vector.tensor_copy(picked_scales[:], scale_table[:].indirect(offsets[:]))
 
         w_grouped = [keep.tile([P, P, PACK], BF16, name="w_grouped%d" % b, align_bytes=64) for b in range(2)]
-        w_codes = [keep.tile([P, P], U32, name="w_codes%d" % b, align_bytes=64) for b in range(2)]
+        w_codes = [keep.tile([P, P], U32, name="w_codes%d" % b, tag=("reused", "w_codes1")[b], align_bytes=64) for b in range(2)]
         w_scales = [keep.tile([P, P], U8, name="w_scales%d" % b, align_bytes=64) for b in range(2)]
         for b in range(2):
             nc.scalar.copy(w_grouped[b][:], w_raw[b][:].rearrange("p j n -> p n j"))

from contextlib import ExitStack

import concourse.mybir as mybir

K, T, S, N = 512, 2048, 1024, 256
FLOPS = 2 * K * S * N

F32 = mybir.dt.float32
BF16 = mybir.dt.bfloat16
I32 = mybir.dt.int32
U32 = mybir.dt.uint32
U16 = mybir.dt.uint16
U8 = mybir.dt.uint8
FP8X4 = mybir.dt.float8_e4m3fn_x4
MULT = mybir.AluOpType.mult

P = 128
PACK = 4
PER_COL = 16
BANK = 512
FIRST = 256


def tile_picked_depth_lin_none_sub_p_kernel(tc, x_words, x_scales, w, gate, offs, out):
    nc = tc.nc
    with ExitStack() as ctx:
        keep = ctx.enter_context(tc.tile_pool(name="keep", bufs=1))
        psum = ctx.enter_context(tc.psum_pool(name="psum", bufs=1))

        offsets = keep.tile([P, S // PER_COL], U16, name="offsets")
        nc.sync.dma_start(offsets[:], offs)

        w_rows = w.rearrange("(p j) n -> p j n", j=PACK)
        w_raw = [keep.tile([P, PACK, P], F32, name="w_raw%d" % b, align_bytes=64) for b in range(2)]
        nc.sync.dma_start(w_raw[0][:], w_rows[:, :, 0:P])

        scale_table = keep.tile([P, T], U8, name="scale_table", tag="reused", align_bytes=64)
        nc.vector.memset(scale_table[:].bitcast(I32), 0)
        for q in range(4):
            nc.sync.dma_start(
                scale_table[32 * q : 32 * q + 4, :].bitcast(I32),
                x_scales[0, 4 * q : 4 * q + 4, :].bitcast(I32),
            )

        word_table = keep.tile([P, T], I32, name="word_table", align_bytes=64)
        nc.sync.dma_start(word_table[:], x_words[0].rearrange("p c r -> p (c r)").bitcast(I32))

        nc.sync.dma_start(w_raw[1][:], w_rows[:, :, P : 2 * P])

        gates = keep.tile([P, S], F32, name="gates", align_bytes=64)
        nc.sync.dma_start(gates[:], gate[0:P, :])

        windows = [keep.tile([P, T], F32, name="window%d" % b, align_bytes=64) for b in range(2)]
        zero = keep.tile([P, 1], F32, name="zero")
        nc.vector.memset(zero[:], 0.0)
        nc.vector.memset(windows[0][:], 0.0)
        nc.scalar.copy(windows[1][:], zero[:].to_broadcast([P, T]))

        picked_scales = keep.tile([P, S], U8, name="picked_scales", align_bytes=64)
        nc.vector.tensor_copy(picked_scales[:], scale_table[:].indirect(offsets[:]))

        w_grouped = [keep.tile([P, P, PACK], BF16, name="w_grouped%d" % b, align_bytes=64) for b in range(2)]
        w_codes = [keep.tile([P, P], U32, name="w_codes%d" % b, tag=("reused", "w_codes1")[b], align_bytes=64) for b in range(2)]
        w_scales = [keep.tile([P, P], U8, name="w_scales%d" % b, align_bytes=64) for b in range(2)]
        for b in range(2):
            nc.scalar.copy(w_grouped[b][:], w_raw[b][:].rearrange("p j n -> p n j"))

        def quantize_w(b):
            nc.vector.quantize_mx(
                out=w_codes[b][:].bitcast(FP8X4),
                scales=w_scales[b][:],
                in_=w_grouped[b][:].rearrange("p n j -> p (n j)"),
            )

        pieces = [(0, FIRST), (FIRST, S)]

        def entries(lo, hi):
            return offsets[:, lo // PER_COL : hi // PER_COL]

        picked_words = keep.tile([P, S], U32, name="picked_words", align_bytes=64)
        quantize_w(0)
        for lo, hi in pieces:
            nc.vector.tensor_copy(picked_words[:, lo:hi], word_table[:].bitcast(U32).indirect(entries(lo, hi)))
        quantize_w(1)

        bank_of = {(0, 0, 0): 0, (0, 1, 0): 1, (1, 0, 0): 1, (1, 0, BANK): 2, (1, 1, 0): 1, (1, 1, BANK): 2}
        y = {}
        for h, (lo, hi) in enumerate(pieces):
            for b in range(2):
                y[h, b] = keep.tile([P, hi - lo], F32, name="y%d%d" % (h, b), align_bytes=64)
                for c0 in range(0, hi - lo, BANK):
                    c1 = min(c0 + BANK, hi - lo)
                    acc = psum.tile([P, c1 - c0], F32, name="acc%d%d%d" % (h, b, c0), tag="bank%d" % bank_of[h, b, c0])
                    nc.tensor.matmul_mx(
                        out=acc[:],
                        lhsT=w_codes[b][:].bitcast(FP8X4),
                        lhsT_scale=w_scales[b][:],
                        rhs=picked_words[:, lo + c0 : lo + c1].bitcast(FP8X4),
                        rhs_scale=picked_scales[:, lo + c0 : lo + c1],
                        start=True,
                        stop=True,
                    )
                    nc.scalar.copy(y[h, b][:, c0:c1], acc[:])

        for h, (lo, hi) in enumerate(pieces):
            for b in range(2):
                nc.vector.tensor_tensor(windows[b][:].indirect(entries(lo, hi)), y[h, b][:], gates[:, lo:hi], MULT)
                if h == len(pieces) - 1:
                    nc.sync.dma_start(out[b * P : (b + 1) * P, :], windows[b][:])
